import numpy as np, ml_dtypes
CORES = [32,160,288,416,80,208,336,464]
N = 8
import mx_ref
NC, G = 128, 2
C = np.float32(0.041)
BF = ml_dtypes.bfloat16
def cut(t, i, w=512):
    return t[:, w * i:w * i + w]
def tile(rs):
    return np.stack(rs, axis=2).reshape(128, -1).astype(BF)
def layer(w, X):
    out = []
    for i in range(G):
        for t in range(len(X)):
            p = mx_ref.matmul(mx_ref.quantize(cut(w, len(X) * i + t)), X[t])
            z = p if t == 0 else z + p
        out.append(z)
    return out
def act(Z):
    return [np.maximum(s * z, 0) * C for z in Z for s in (1, -1)]
def setup_inputs(rng):
    def f(*shape):
        return mx_ref.flush((rng.standard_normal(shape, dtype=np.float32) * np.exp2(rng.integers(-2, 3, shape[:-1] + (1,)))).astype(BF))
    return {"x": f(N, 128, 4 * NC), "w1": f(N, 128, G * 512), "w2": f(N, 128, 512)}
def setup_inputs_blocks(rng):
    d = setup_inputs(rng)
    for k in ("x", "w1", "w2"): d[k] = mx_ref.spread(d[k], rng, 4)
    return d
def setup_inputs_wide(rng):
    d = setup_inputs(rng)
    for k in ("x", "w1", "w2"): d[k] = mx_ref.flush((d[k].astype(np.float32) * np.exp2(rng.integers(-8, 9, (N, 1, 1))).astype(np.float32)).astype(BF))
    return d
def setup_inputs_zeros(rng):
    d = setup_inputs(rng); v = d["x"].reshape(N, 128, -1, 4).copy()
    v[np.broadcast_to((rng.random((N, 1, v.shape[2], 1)) < 0.33), v.shape)] = 0
    d["x"] = v.reshape(d["x"].shape)
    return d
def reference(x, w1, w2):
    H = [mx_ref.quantize(tile(act(layer(w1[j], [mx_ref.quantize(x[j])])))) for j in range(N)]
    y = np.full((N, 128, N * NC), np.nan, np.float32)
    for r in range(N):
        qw = mx_ref.quantize(w2[r])
        for j in range(r + 1):
            y[r][:, NC * j:NC * j + NC] = mx_ref.matmul(qw, H[j])
    return {"y": y}

@@ -1,0 +1,210 @@
+import numpy as np
+from concourse.bass import DstId, RemoteDMATransfer
+from concourse.mybir import dt, AluOpType, ActivationFunctionType
+
+N = 8
+NC = 128
+TW = 4 * NC
+BANK = 512
+C = float(np.float32(0.041))
+
+SCRATCH = {
+    "xb": ("sbuf", [128, TW], "bfloat16"),
+    "w1b": ("sbuf", [128, 2 * TW], "bfloat16"),
+    "w2b": ("sbuf", [128, TW], "bfloat16"),
+    "hb": ("sbuf", [128, TW], "bfloat16"),
+    "xq": ("sbuf", [128, NC], "float8_e4m3fn_x4"),
+    "xs": ("sbuf", [128, NC], "uint8"),
+    "w1q": ("sbuf", [128, 2 * NC], "float8_e4m3fn_x4"),
+    "w1s": ("sbuf", [128, 2 * NC], "uint8"),
+    "w2q": ("sbuf", [128, NC], "float8_e4m3fn_x4"),
+    "w2s": ("sbuf", [128, NC], "uint8"),
+    "hq": ("sbuf", [128, N * NC], "float8_e4m3fn_x4"),
+    "hs": ("sbuf", [128, N * NC], "uint8"),
+    "ysb": ("sbuf", [128, N * NC], "float32"),
+    "ps": ("psum", [128, 8 * BANK], "float32"),
+}
+SEMAPHORES = (["lx", "la", "lb", "lw", "qx", "qa", "qb", "qw", "z0", "z1", "act", "hqd", "sent", "sts", "sta"]
+              + ["c%d" % j for j in range(N)] + ["p%d" % j for j in range(N)]
+              + ["m%d" % k for k in range(N)] + ["v%d" % k for k in range(N)])
+
+_CACHE = {}
+
+
+def _links(topo, a, b):
+    if topo.mates(a, b) or topo.same_plane(a, b):
+        return 1
+    if topo.rack(topo.host(a)) != topo.rack(topo.host(b)) and topo.chip(a) == topo.chip(b):
+        return 1
+    return 2
+
+
+def _plan(cores, topo):
+    n = len(cores)
+
+    def ok(a, b):
+        return topo.may_write(cores[a], cores[b])
+
+    def far_cable(a, b):
+        return topo.rack(topo.host(cores[a])) != topo.rack(topo.host(cores[b])) and _links(topo, cores[a], cores[b]) == 1
+
+    hop = 2.0
+    direct = [[r for r in range(j + 1, n) if ok(j, r)] for j in range(n)]
+    load = [max(len(d), 1 + hop) for d in direct]
+    passes = [{} for _ in range(n)]
+    for j in range(n):
+        for r in range(j + 1, n):
+            if ok(j, r):
+                continue
+            cand = [k for k in direct[j] if direct[k] and ok(k, r)]
+            k = min(cand, key=lambda k: (_links(topo, cores[j], cores[k]) + _links(topo, cores[k], cores[r]),
+                                         0 if far_cable(k, r) else 1, load[k], k))
+            load[k] += 1
+            passes[k].setdefault(j, []).append(r)
+    own, src, eta, free = [], {}, {}, []
+    for j in range(n):
+        first = sorted([k for k in direct[j] if j in passes[k]], key=lambda k: (len(direct[k]), k))
+        rest = [r for r in direct[j] if r not in first]
+        groups = [[k] for k in first] + ([rest] if rest else [])
+        t = 0.0
+        for grp in groups:
+            t += len(grp)
+            for r in grp:
+                src[(r, j)] = (j, grp)
+                eta[(r, j)] = t + hop
+        own.append(groups)
+        free.append(t)
+    fwd = []
+    for k in range(n):
+        todo = sorted(passes[k].items(), key=lambda it: (eta[(k, it[0])], it[0]))
+        t = free[k]
+        for j, grp in todo:
+            t = max(t, eta[(k, j)]) + len(grp)
+            for r in grp:
+                src[(r, j)] = (k, grp)
+                eta[(r, j)] = t + hop
+        fwd.append(todo)
+    order = [[r] + sorted(range(r), key=lambda j: (eta[(r, j)], j)) for r in range(n)]
+    return {"own": own, "fwd": fwd, "src": src, "order": order}
+
+
+def _mask(topo, cores, k, grp):
+    m = topo.mask(cores[k], cores[grp[0]])
+    for r in grp[1:]:
+        m &= topo.mask(cores[k], cores[r])
+    return m
+
+
+def _engines(mask):
+    return bin(mask).count("1")
+
+
+def rank_program(g, core, T, topo):
+    rank = T.rank_of(core)
+    if rank is None:
+        return
+    cores = list(T.cores)
+    if "plan" not in _CACHE:
+        _CACHE["plan"] = _plan(cores, topo)
+    plan = _CACHE["plan"]
+    S = T.sem
+    Relu, Copy = ActivationFunctionType.Relu, ActivationFunctionType.Copy
+
+    def blk(j):
+        return slice(NC * j, NC * (j + 1))
+
+    g.sync.dma_start(T.xb[:], T.x[:]).then_inc(S.lx, 16)
+    g.scalar.dma_start(T.w1b[:, 0:TW], T.w1[:, 0:TW]).then_inc(S.la, 16)
+    g.sync.dma_start(T.w1b[:, TW:2 * TW], T.w1[:, TW:2 * TW]).then_inc(S.lb, 16)
+    g.sync.wait_ge(S.lx, 16)
+    g.sync.wait_ge(S.la, 16)
+    g.sync.wait_ge(S.lb, 16)
+    g.sync.dma_start(T.w2b[:], T.w2[:]).then_inc(S.lw, 16)
+
+    g.vector.wait_ge(S.lx, 16)
+    g.vector.quantize_mx(T.xq[:], T.xs[:], T.xb[:]).then_inc(S.qx, 1)
+    g.vector.wait_ge(S.la, 16)
+    g.vector.quantize_mx(T.w1q[:, 0:NC], T.w1s[:, 0:NC], T.w1b[:, 0:TW]).then_inc(S.qa, 1)
+    g.vector.wait_ge(S.lb, 16)
+    g.vector.quantize_mx(T.w1q[:, NC:2 * NC], T.w1s[:, NC:2 * NC], T.w1b[:, TW:2 * TW]).then_inc(S.qb, 1)
+
+    g.tensor.wait_ge(S.qx, 1)
+    g.tensor.wait_ge(S.qa, 1)
+    g.tensor.matmul_mx(T.ps[:, 0:NC], T.w1q[:, 0:NC], T.w1s[:, 0:NC], T.xq[:], T.xs[:], True, True).then_inc(S.z0, 1)
+    g.tensor.wait_ge(S.qb, 1)
+    g.tensor.matmul_mx(T.ps[:, BANK:BANK + NC], T.w1q[:, NC:2 * NC], T.w1s[:, NC:2 * NC], T.xq[:], T.xs[:], True, True).then_inc(S.z1, 1)
+
+    g.scalar.wait_ge(S.z0, 1)
+    g.scalar.activation(T.hb[:, 0:TW:4], T.ps[:, 0:NC], Relu, scale=C).then_inc(S.act, 1)
+    g.scalar.activation(T.hb[:, 1:TW:4], T.ps[:, 0:NC], Relu, scale=-C).then_inc(S.act, 1)
+    g.vector.wait_ge(S.z1, 1)
+    g.vector.tensor_scalar(T.hb[:, 2:TW:4], T.ps[:, BANK:BANK + NC], C, 0.0, AluOpType.mult, AluOpType.max).then_inc(S.act, 1)
+    g.vector.tensor_scalar(T.hb[:, 3:TW:4], T.ps[:, BANK:BANK + NC], -C, 0.0, AluOpType.mult, AluOpType.max).then_inc(S.act, 1)
+    g.vector.wait_ge(S.act, 4)
+    g.vector.quantize_mx(T.hq[:, blk(rank)], T.hs[:, blk(rank)], T.hb[:]).then_inc(S.hqd, 1)
+    g.vector.wait_ge(S.lw, 16)
+    g.vector.quantize_mx(T.w2q[:], T.w2s[:], T.w2b[:]).then_inc(S.qw, 1)
+
+    sent = [0]
+
+    def send(j, grp, codes):
+        mask = _mask(topo, cores, rank, grp)
+        sem = S["c%d" % j] if codes else S["p%d" % j]
+
+        def view():
+            return T.hq[:, blk(j)].bitcast(dt.uint8) if codes else T.hs[:, blk(j)]
+
+        where = [topo.addr(cores[r], core) for r in grp]
+        if len(grp) == 1:
+            g.remote_dma(out_ap=view(), in_ap=view(), remote_sem=sem, local_sem=S.sent,
+                         pid=where[0][1], routing_id=where[0][0], dma_engine_mask=mask)
+        else:
+            g.remote_dma_fused([RemoteDMATransfer(dst_ids=[DstId(rid=a, pnc=p) for a, p in where], dma_engine_mask=mask,
+                                                  remote_sem=sem, srcs=[view()], dsts=[view() for _ in grp], alu_op=0)],
+                               local_sem=S.sent)
+        sent[0] += _engines(mask)
+
+    def landed(j):
+        k, grp = plan["src"][(rank, j)]
+        return _engines(_mask(topo, cores, k, grp))
+
+    if plan["own"][rank]:
+        g.wait_ge(S.hqd, 1)
+    for grp in plan["own"][rank]:
+        send(rank, grp, True)
+        send(rank, grp, False)
+    for j, grp in plan["fwd"][rank]:
+        g.wait_ge(S["c%d" % j], landed(j))
+        send(j, grp, True)
+        g.wait_ge(S["p%d" % j], landed(j))
+        send(j, grp, False)
+
+    g.tensor.wait_ge(S.qw, 1)
+    stores = {"sts": 0, "sta": 0}
+    for k, j in enumerate(plan["order"][rank]):
+        bank = (k + 2) % 8
+        out = T.ps[:, BANK * bank:BANK * bank + NC]
+        if j == rank:
+            g.tensor.wait_ge(S.hqd, 1)
+        else:
+            g.tensor.wait_ge(S["c%d" % j], landed(j))
+            g.tensor.wait_ge(S["p%d" % j], landed(j))
+        g.tensor.matmul_mx(out, T.w2q[:], T.w2s[:], T.hq[:, blk(j)], T.hs[:, blk(j)], True, True).then_inc(S["m%d" % k], 1)
+        if k % 2 == 0:
+            g.vector.wait_ge(S["m%d" % k], 1)
+            g.vector.tensor_copy(T.ysb[:, blk(j)], out).then_inc(S["v%d" % k], 1)
+            g.sync.wait_ge(S["v%d" % k], 1)
+            g.sync.dma_start(T.y[:, blk(j)], T.ysb[:, blk(j)]).then_inc(S.sts, 16)
+            stores["sts"] += 16
+        else:
+            g.scalar.wait_ge(S["m%d" % k], 1)
+            g.scalar.activation(T.ysb[:, blk(j)], out, Copy).then_inc(S["v%d" % k], 1)
+            g.scalar.wait_ge(S["v%d" % k], 1)
+            g.scalar.dma_start(T.y[:, blk(j)], T.ysb[:, blk(j)]).then_inc(S.sta, 16)
+            stores["sta"] += 16
+
+    if sent[0]:
+        g.wait_ge(S.sent, sent[0])
+    for name, total in stores.items():
+        if total:
+            g.wait_ge(S[name], total)

@@ -7,6 +7,7 @@ NC = 128
 TW = 4 * NC
 BANK = 512
 C = float(np.float32(0.041))
+HEAVY = 3
 
 SCRATCH = {
     "xb": ("sbuf", [128, TW], "bfloat16"),
@@ -39,8 +40,18 @@ def _links(topo, a, b):
     return 2
 
 
+def _helper(topo, c, readers, total):
+    for h in range(total):
+        if (topo.host(h) == topo.host(c) and topo.chip(h) == topo.chip(c) and topo.die(h) != topo.die(c)
+                and topo.may_write(c, h) and all(topo.may_write(h, r) for r in readers)):
+            return h
+    return None
+
+
 def _plan(cores, topo):
     n = len(cores)
+    ext = list(cores)
+    total = (max(topo.host(c) for c in cores) + 1) * topo.CORES_PER_HOST
 
     def ok(a, b):
         return topo.may_write(cores[a], cores[b])
@@ -50,15 +61,15 @@ def _plan(cores, topo):
 
     hop = 2.0
     direct = [[r for r in range(j + 1, n) if ok(j, r)] for j in range(n)]
-    load = [max(len(d), 1 + hop) for d in direct]
+    load = [len(direct[j]) if len(direct[j]) < HEAVY else 1 + (n - 1 - j - len(direct[j])) for j in range(n)]
     passes = [{} for _ in range(n)]
     for j in range(n):
         for r in range(j + 1, n):
             if ok(j, r):
                 continue
-            cand = [k for k in direct[j] if direct[k] and ok(k, r)]
+            cand = [k for k in direct[j] if ok(k, r)]
             k = min(cand, key=lambda k: (_links(topo, cores[j], cores[k]) + _links(topo, cores[k], cores[r]),
-                                         0 if far_cable(k, r) else 1, load[k], k))
+                                         load[k], 0 if far_cable(k, r) else 1, k))
             load[k] += 1
             passes[k].setdefault(j, []).append(r)
     own, src, eta, free = [], {}, {}, []
@@ -66,6 +77,11 @@ def _plan(cores, topo):
         first = sorted([k for k in direct[j] if j in passes[k]], key=lambda k: (len(direct[k]), k))
         rest = [r for r in direct[j] if r not in first]
         groups = [[k] for k in first] + ([rest] if rest else [])
+        h = _helper(topo, cores[j], [cores[r] for r in rest], total) if (rest and len(direct[j]) >= HEAVY) else None
+        if h is not None:
+            groups = [[len(ext)]] + [[k] for k in first]
+            ext.append(h)
+            passes.append({j: rest})
         t = 0.0
         for grp in groups:
             t += len(grp)
@@ -75,7 +91,10 @@ def _plan(cores, topo):
         own.append(groups)
         free.append(t)
     fwd = []
-    for k in range(n):
+    for k in range(len(ext)):
+        if k >= n:
+            own.append([])
+            free.append(0.0)
         todo = sorted(passes[k].items(), key=lambda it: (eta[(k, it[0])], it[0]))
         t = free[k]
         for j, grp in todo:
@@ -84,15 +103,15 @@ def _plan(cores, topo):
                 src[(r, j)] = (k, grp)
                 eta[(r, j)] = t + hop
         fwd.append(todo)
-    order = [[r] + sorted(range(r), key=lambda j: (eta[(r, j)], j)) for r in range(n)]
-    return {"own": own, "fwd": fwd, "src": src, "order": order}
-
-
-def _mask(topo, cores, k, grp):
-    m = topo.mask(cores[k], cores[grp[0]])
-    for r in grp[1:]:
-        m &= topo.mask(cores[k], cores[r])
-    return m
+    order = [[r] + sorted(range(r), key=lambda j: (src[(r, j)][0] != j, eta[(r, j)], j)) for r in range(n)]
+    eng = []
+    for k in range(len(ext)):
+        m = -1
+        for grp in own[k] + [grp for _, grp in fwd[k]]:
+            for r in grp:
+                m &= topo.mask(ext[k], ext[r])
+        eng.append(m)
+    return {"own": own, "fwd": fwd, "src": src, "order": order, "ext": ext, "eng": eng}
 
 
 def _engines(mask):
@@ -100,61 +119,63 @@ def _engines(mask):
 
 
 def rank_program(g, core, T, topo):
-    rank = T.rank_of(core)
-    if rank is None:
-        return
-    cores = list(T.cores)
     if "plan" not in _CACHE:
-        _CACHE["plan"] = _plan(cores, topo)
+        _CACHE["plan"] = _plan(list(T.cores), topo)
     plan = _CACHE["plan"]
+    ext = plan["ext"]
+    if core not in ext:
+        return
+    rank = ext.index(core)
+    works = rank < N
     S = T.sem
     Relu, Copy = ActivationFunctionType.Relu, ActivationFunctionType.Copy
 
     def blk(j):
         return slice(NC * j, NC * (j + 1))
 
-    g.sync.dma_start(T.xb[:], T.x[:]).then_inc(S.lx, 16)
-    g.scalar.dma_start(T.w1b[:, 0:TW], T.w1[:, 0:TW]).then_inc(S.la, 16)
-    g.sync.dma_start(T.w1b[:, TW:2 * TW], T.w1[:, TW:2 * TW]).then_inc(S.lb, 16)
-    g.sync.wait_ge(S.lx, 16)
-    g.sync.wait_ge(S.la, 16)
-    g.sync.wait_ge(S.lb, 16)
-    g.sync.dma_start(T.w2b[:], T.w2[:]).then_inc(S.lw, 16)
+    if works:
+        g.sync.dma_start(T.xb[:], T.x[:]).then_inc(S.lx, 16)
+        g.scalar.dma_start(T.w1b[:, 0:TW], T.w1[:, 0:TW]).then_inc(S.la, 16)
+        g.sync.dma_start(T.w1b[:, TW:2 * TW], T.w1[:, TW:2 * TW]).then_inc(S.lb, 16)
+        g.sync.wait_ge(S.lx, 16)
+        g.sync.wait_ge(S.la, 16)
+        g.sync.wait_ge(S.lb, 16)
+        g.sync.dma_start(T.w2b[:], T.w2[:]).then_inc(S.lw, 16)
 
-    g.vector.wait_ge(S.lx, 16)
-    g.vector.quantize_mx(T.xq[:], T.xs[:], T.xb[:]).then_inc(S.qx, 1)
-    g.vector.wait_ge(S.la, 16)
-    g.vector.quantize_mx(T.w1q[:, 0:NC], T.w1s[:, 0:NC], T.w1b[:, 0:TW]).then_inc(S.qa, 1)
-    g.vector.wait_ge(S.lb, 16)
-    g.vector.quantize_mx(T.w1q[:, NC:2 * NC], T.w1s[:, NC:2 * NC], T.w1b[:, TW:2 * TW]).then_inc(S.qb, 1)
+        g.vector.wait_ge(S.lx, 16)
+        g.vector.quantize_mx(T.xq[:], T.xs[:], T.xb[:]).then_inc(S.qx, 1)
+        g.vector.wait_ge(S.la, 16)
+        g.vector.quantize_mx(T.w1q[:, 0:NC], T.w1s[:, 0:NC], T.w1b[:, 0:TW]).then_inc(S.qa, 1)
+        g.vector.wait_ge(S.lb, 16)
+        g.vector.quantize_mx(T.w1q[:, NC:2 * NC], T.w1s[:, NC:2 * NC], T.w1b[:, TW:2 * TW]).then_inc(S.qb, 1)
 
-    g.tensor.wait_ge(S.qx, 1)
-    g.tensor.wait_ge(S.qa, 1)
-    g.tensor.matmul_mx(T.ps[:, 0:NC], T.w1q[:, 0:NC], T.w1s[:, 0:NC], T.xq[:], T.xs[:], True, True).then_inc(S.z0, 1)
-    g.tensor.wait_ge(S.qb, 1)
-    g.tensor.matmul_mx(T.ps[:, BANK:BANK + NC], T.w1q[:, NC:2 * NC], T.w1s[:, NC:2 * NC], T.xq[:], T.xs[:], True, True).then_inc(S.z1, 1)
+        g.tensor.wait_ge(S.qx, 1)
+        g.tensor.wait_ge(S.qa, 1)
+        g.tensor.matmul_mx(T.ps[:, 0:NC], T.w1q[:, 0:NC], T.w1s[:, 0:NC], T.xq[:], T.xs[:], True, True).then_inc(S.z0, 1)
+        g.tensor.wait_ge(S.qb, 1)
+        g.tensor.matmul_mx(T.ps[:, BANK:BANK + NC], T.w1q[:, NC:2 * NC], T.w1s[:, NC:2 * NC], T.xq[:], T.xs[:], True, True).then_inc(S.z1, 1)
 
-    g.scalar.wait_ge(S.z0, 1)
-    g.scalar.activation(T.hb[:, 0:TW:4], T.ps[:, 0:NC], Relu, scale=C).then_inc(S.act, 1)
-    g.scalar.activation(T.hb[:, 1:TW:4], T.ps[:, 0:NC], Relu, scale=-C).then_inc(S.act, 1)
-    g.vector.wait_ge(S.z1, 1)
-    g.vector.tensor_scalar(T.hb[:, 2:TW:4], T.ps[:, BANK:BANK + NC], C, 0.0, AluOpType.mult, AluOpType.max).then_inc(S.act, 1)
-    g.vector.tensor_scalar(T.hb[:, 3:TW:4], T.ps[:, BANK:BANK + NC], -C, 0.0, AluOpType.mult, AluOpType.max).then_inc(S.act, 1)
-    g.vector.wait_ge(S.act, 4)
-    g.vector.quantize_mx(T.hq[:, blk(rank)], T.hs[:, blk(rank)], T.hb[:]).then_inc(S.hqd, 1)
-    g.vector.wait_ge(S.lw, 16)
-    g.vector.quantize_mx(T.w2q[:], T.w2s[:], T.w2b[:]).then_inc(S.qw, 1)
+        g.scalar.wait_ge(S.z0, 1)
+        g.scalar.activation(T.hb[:, 0:TW:4], T.ps[:, 0:NC], Relu, scale=C).then_inc(S.act, 1)
+        g.scalar.activation(T.hb[:, 1:TW:4], T.ps[:, 0:NC], Relu, scale=-C).then_inc(S.act, 1)
+        g.vector.wait_ge(S.z1, 1)
+        g.vector.tensor_scalar(T.hb[:, 2:TW:4], T.ps[:, BANK:BANK + NC], C, 0.0, AluOpType.mult, AluOpType.max).then_inc(S.act, 1)
+        g.vector.tensor_scalar(T.hb[:, 3:TW:4], T.ps[:, BANK:BANK + NC], -C, 0.0, AluOpType.mult, AluOpType.max).then_inc(S.act, 1)
+        g.vector.wait_ge(S.act, 4)
+        g.vector.quantize_mx(T.hq[:, blk(rank)], T.hs[:, blk(rank)], T.hb[:]).then_inc(S.hqd, 1)
+        g.vector.wait_ge(S.lw, 16)
+        g.vector.quantize_mx(T.w2q[:], T.w2s[:], T.w2b[:]).then_inc(S.qw, 1)
 
     sent = [0]
 
     def send(j, grp, codes):
-        mask = _mask(topo, cores, rank, grp)
+        mask = plan["eng"][rank]
         sem = S["c%d" % j] if codes else S["p%d" % j]
 
         def view():
             return T.hq[:, blk(j)].bitcast(dt.uint8) if codes else T.hs[:, blk(j)]
 
-        where = [topo.addr(cores[r], core) for r in grp]
+        where = [topo.addr(ext[r], core) for r in grp]
         if len(grp) == 1:
             g.remote_dma(out_ap=view(), in_ap=view(), remote_sem=sem, local_sem=S.sent,
                          pid=where[0][1], routing_id=where[0][0], dma_engine_mask=mask)
@@ -165,8 +186,7 @@ def rank_program(g, core, T, topo):
         sent[0] += _engines(mask)
 
     def landed(j):
-        k, grp = plan["src"][(rank, j)]
-        return _engines(_mask(topo, cores, k, grp))
+        return _engines(plan["eng"][plan["src"][(rank, j)][0]])
 
     if plan["own"][rank]:
         g.wait_ge(S.hqd, 1)
@@ -179,29 +199,30 @@ def rank_program(g, core, T, topo):
         g.wait_ge(S["p%d" % j], landed(j))
         send(j, grp, False)
 
-    g.tensor.wait_ge(S.qw, 1)
     stores = {"sts": 0, "sta": 0}
-    for k, j in enumerate(plan["order"][rank]):
-        bank = (k + 2) % 8
-        out = T.ps[:, BANK * bank:BANK * bank + NC]
-        if j == rank:
-            g.tensor.wait_ge(S.hqd, 1)
-        else:
-            g.tensor.wait_ge(S["c%d" % j], landed(j))
-            g.tensor.wait_ge(S["p%d" % j], landed(j))
-        g.tensor.matmul_mx(out, T.w2q[:], T.w2s[:], T.hq[:, blk(j)], T.hs[:, blk(j)], True, True).then_inc(S["m%d" % k], 1)
-        if k % 2 == 0:
-            g.vector.wait_ge(S["m%d" % k], 1)
-            g.vector.tensor_copy(T.ysb[:, blk(j)], out).then_inc(S["v%d" % k], 1)
-            g.sync.wait_ge(S["v%d" % k], 1)
-            g.sync.dma_start(T.y[:, blk(j)], T.ysb[:, blk(j)]).then_inc(S.sts, 16)
-            stores["sts"] += 16
-        else:
-            g.scalar.wait_ge(S["m%d" % k], 1)
-            g.scalar.activation(T.ysb[:, blk(j)], out, Copy).then_inc(S["v%d" % k], 1)
-            g.scalar.wait_ge(S["v%d" % k], 1)
-            g.scalar.dma_start(T.y[:, blk(j)], T.ysb[:, blk(j)]).then_inc(S.sta, 16)
-            stores["sta"] += 16
+    if works:
+        g.tensor.wait_ge(S.qw, 1)
+        for k, j in enumerate(plan["order"][rank]):
+            bank = (k + 2) % 8
+            out = T.ps[:, BANK * bank:BANK * bank + NC]
+            if j == rank:
+                g.tensor.wait_ge(S.hqd, 1)
+            else:
+                g.tensor.wait_ge(S["c%d" % j], landed(j))
+                g.tensor.wait_ge(S["p%d" % j], landed(j))
+            g.tensor.matmul_mx(out, T.w2q[:], T.w2s[:], T.hq[:, blk(j)], T.hs[:, blk(j)], True, True).then_inc(S["m%d" % k], 1)
+            if k % 2 == 0:
+                g.vector.wait_ge(S["m%d" % k], 1)
+                g.vector.tensor_copy(T.ysb[:, blk(j)], out).then_inc(S["v%d" % k], 1)
+                g.sync.wait_ge(S["v%d" % k], 1)
+                g.sync.dma_start(T.y[:, blk(j)], T.ysb[:, blk(j)]).then_inc(S.sts, 16)
+                stores["sts"] += 16
+            else:
+                g.scalar.wait_ge(S["m%d" % k], 1)
+                g.scalar.activation(T.ysb[:, blk(j)], out, Copy).then_inc(S["v%d" % k], 1)
+                g.scalar.wait_ge(S["v%d" % k], 1)
+                g.scalar.dma_start(T.y[:, blk(j)], T.ysb[:, blk(j)]).then_inc(S.sta, 16)
+                stores["sta"] += 16
 
     if sent[0]:
         g.wait_ge(S.sent, sent[0])

@@ -7,7 +7,6 @@ NC = 128
 TW = 4 * NC
 BANK = 512
 C = float(np.float32(0.041))
-HEAVY = 3
 
 SCRATCH = {
     "xb": ("sbuf", [128, TW], "bfloat16"),
@@ -56,32 +55,36 @@ def _plan(cores, topo):
     def ok(a, b):
         return topo.may_write(cores[a], cores[b])
 
-    def far_cable(a, b):
-        return topo.rack(topo.host(cores[a])) != topo.rack(topo.host(cores[b])) and _links(topo, cores[a], cores[b]) == 1
+    def rk(a):
+        return topo.rack(topo.host(cores[a]))
 
     hop = 2.0
-    direct = [[r for r in range(j + 1, n) if ok(j, r)] for j in range(n)]
-    load = [len(direct[j]) if len(direct[j]) < HEAVY else 1 + (n - 1 - j - len(direct[j])) for j in range(n)]
+    late = 1.0
     passes = [{} for _ in range(n)]
+    gate, others = [], []
     for j in range(n):
-        for r in range(j + 1, n):
-            if ok(j, r):
-                continue
-            cand = [k for k in direct[j] if ok(k, r)]
-            k = min(cand, key=lambda k: (_links(topo, cores[j], cores[k]) + _links(topo, cores[k], cores[r]),
-                                         load[k], 0 if far_cable(k, r) else 1, k))
-            load[k] += 1
-            passes[k].setdefault(j, []).append(r)
+        direct = [r for r in range(j + 1, n) if ok(j, r)]
+        refused = [r for r in range(j + 1, n) if not ok(j, r)]
+        gt = None
+        if refused:
+            cand = [k for k in direct if all(ok(k, r) and rk(k) == rk(r) for r in refused)]
+            gt = min(cand, key=lambda k: (_links(topo, cores[j], cores[k]), k))
+            passes[gt][j] = refused
+        gate.append(gt)
+        others.append([r for r in direct if r != gt])
     own, src, eta, free = [], {}, {}, []
     for j in range(n):
-        first = sorted([k for k in direct[j] if j in passes[k]], key=lambda k: (len(direct[k]), k))
-        rest = [r for r in direct[j] if r not in first]
-        groups = [[k] for k in first] + ([rest] if rest else [])
-        h = _helper(topo, cores[j], [cores[r] for r in rest], total) if (rest and len(direct[j]) >= HEAVY) else None
-        if h is not None:
-            groups = [[len(ext)]] + [[k] for k in first]
-            ext.append(h)
-            passes.append({j: rest})
+        first = [[gate[j]]] if gate[j] is not None else []
+        rest = list(others[j])
+        groups = first + ([rest] if rest else [])
+        if len(rest) >= 2:
+            keep = [min(rest)] if (not passes[j] and len(rest) > 2) else []
+            rest = [r for r in rest if r not in keep]
+            h = _helper(topo, cores[j], [cores[r] for r in rest], total)
+            if h is not None:
+                groups = [[len(ext)]] + first + [[k] for k in keep]
+                ext.append(h)
+                passes.append({j: rest})
         t = 0.0
         for grp in groups:
             t += len(grp)
@@ -97,13 +100,13 @@ def _plan(cores, topo):
             free.append(0.0)
         todo = sorted(passes[k].items(), key=lambda it: (eta[(k, it[0])], it[0]))
         t = free[k]
-        for j, grp in todo:
-            t = max(t, eta[(k, j)]) + len(grp)
+        for i, (j, grp) in enumerate(todo):
+            t = max(t, eta[(k, j)]) + len(grp) + (late if (i == 0 and not own[k]) else 0.0)
             for r in grp:
                 src[(r, j)] = (k, grp)
                 eta[(r, j)] = t + hop
         fwd.append(todo)
-    order = [[r] + sorted(range(r), key=lambda j: (src[(r, j)][0] != j, eta[(r, j)], j)) for r in range(n)]
+    order = [[r] + sorted(range(r), key=lambda j: (eta[(r, j)], j)) for r in range(n)]
     eng = []
     for k in range(len(ext)):
         m = -1
@@ -191,13 +194,13 @@ def rank_program(g, core, T, topo):
     if plan["own"][rank]:
         g.wait_ge(S.hqd, 1)
     for grp in plan["own"][rank]:
-        send(rank, grp, True)
         send(rank, grp, False)
+        send(rank, grp, True)
     for j, grp in plan["fwd"][rank]:
-        g.wait_ge(S["c%d" % j], landed(j))
-        send(j, grp, True)
         g.wait_ge(S["p%d" % j], landed(j))
         send(j, grp, False)
+        g.wait_ge(S["c%d" % j], landed(j))
+        send(j, grp, True)
 
     stores = {"sts": 0, "sta": 0}
     if works:
@@ -208,8 +211,8 @@ def rank_program(g, core, T, topo):
             if j == rank:
                 g.tensor.wait_ge(S.hqd, 1)
             else:
-                g.tensor.wait_ge(S["c%d" % j], landed(j))
                 g.tensor.wait_ge(S["p%d" % j], landed(j))
+                g.tensor.wait_ge(S["c%d" % j], landed(j))
             g.tensor.matmul_mx(out, T.w2q[:], T.w2s[:], T.hq[:, blk(j)], T.hs[:, blk(j)], True, True).then_inc(S["m%d" % k], 1)
             if k % 2 == 0:
                 g.vector.wait_ge(S["m%d" % k], 1)

import numpy as np
from concourse.bass import DstId, RemoteDMATransfer
from concourse.mybir import dt, AluOpType, ActivationFunctionType

N = 8
NC = 128
TW = 4 * NC
BANK = 512
C = float(np.float32(0.041))

SCRATCH = {
    "xb": ("sbuf", [128, TW], "bfloat16"),
    "w1b": ("sbuf", [128, 2 * TW], "bfloat16"),
    "w2b": ("sbuf", [128, TW], "bfloat16"),
    "hb": ("sbuf", [128, TW], "bfloat16"),
    "xq": ("sbuf", [128, NC], "float8_e4m3fn_x4"),
    "xs": ("sbuf", [128, NC], "uint8"),
    "w1q": ("sbuf", [128, 2 * NC], "float8_e4m3fn_x4"),
    "w1s": ("sbuf", [128, 2 * NC], "uint8"),
    "w2q": ("sbuf", [128, NC], "float8_e4m3fn_x4"),
    "w2s": ("sbuf", [128, NC], "uint8"),
    "hq": ("sbuf", [128, N * NC], "float8_e4m3fn_x4"),
    "hs": ("sbuf", [128, N * NC], "uint8"),
    "ysb": ("sbuf", [128, N * NC], "float32"),
    "ps": ("psum", [128, 8 * BANK], "float32"),
}
SEMAPHORES = (["lx", "la", "lb", "lw", "qx", "qa", "qb", "qw", "z0", "z1", "act", "hqd", "sent", "sts", "sta"]
              + ["c%d" % j for j in range(N)] + ["p%d" % j for j in range(N)]
              + ["m%d" % k for k in range(N)] + ["v%d" % k for k in range(N)])

_CACHE = {}


def _links(topo, a, b):
    if topo.mates(a, b) or topo.same_plane(a, b):
        return 1
    if topo.rack(topo.host(a)) != topo.rack(topo.host(b)) and topo.chip(a) == topo.chip(b):
        return 1
    return 2


def _helper(topo, c, readers, total):
    for h in range(total):
        if (topo.host(h) == topo.host(c) and topo.chip(h) == topo.chip(c) and topo.die(h) != topo.die(c)
                and topo.may_write(c, h) and all(topo.may_write(h, r) for r in readers)):
            return h
    return None


def _plan(cores, topo):
    n = len(cores)
    ext = list(cores)
    total = (max(topo.host(c) for c in cores) + 1) * topo.CORES_PER_HOST

    def ok(a, b):
        return topo.may_write(cores[a], cores[b])

    def rk(a):
        return topo.rack(topo.host(cores[a]))

    hop = 2.0
    late = 1.0
    passes = [{} for _ in range(n)]
    gate, others = [], []
    for j in range(n):
        direct = [r for r in range(j + 1, n) if ok(j, r)]
        refused = [r for r in range(j + 1, n) if not ok(j, r)]
        gt = None
        if refused:
            cand = [k for k in direct if all(ok(k, r) and rk(k) == rk(r) for r in refused)]
            gt = min(cand, key=lambda k: (_links(topo, cores[j], cores[k]), k))
            passes[gt][j] = refused
        gate.append(gt)
        others.append([r for r in direct if r != gt])
    own, src, eta, free = [], {}, {}, []
    for j in range(n):
        first = [[gate[j]]] if gate[j] is not None else []
        rest = list(others[j])
        groups = first + ([rest] if rest else [])
        if len(rest) >= 2:
            keep = [min(rest)] if (not passes[j] and len(rest) > 2) else []
            rest = [r for r in rest if r not in keep]
            h = _helper(topo, cores[j], [cores[r] for r in rest], total)
            if h is not None:
                groups = [[len(ext)]] + first + [[k] for k in keep]
                ext.append(h)
                passes.append({j: rest})
        t = 0.0
        for grp in groups:
            t += len(grp)
            for r in grp:
                src[(r, j)] = (j, grp)
                eta[(r, j)] = t + hop
        own.append(groups)
        free.append(t)
    fwd = []
    for k in range(len(ext)):
        if k >= n:
            own.append([])
            free.append(0.0)
        todo = sorted(passes[k].items(), key=lambda it: (eta[(k, it[0])], it[0]))
        t = free[k]
        for i, (j, grp) in enumerate(todo):
            t = max(t, eta[(k, j)]) + len(grp) + (late if (i == 0 and not own[k]) else 0.0)
            for r in grp:
                src[(r, j)] = (k, grp)
                eta[(r, j)] = t + hop
        fwd.append(todo)
    order = [[r] + sorted(range(r), key=lambda j: (eta[(r, j)], j)) for r in range(n)]
    eng = []
    for k in range(len(ext)):
        m = -1
        for grp in own[k] + [grp for _, grp in fwd[k]]:
            for r in grp:
                m &= topo.mask(ext[k], ext[r])
        eng.append(m)
    return {"own": own, "fwd": fwd, "src": src, "order": order, "ext": ext, "eng": eng}


def _engines(mask):
    return bin(mask).count("1")


def rank_program(g, core, T, topo):
    if "plan" not in _CACHE:
        _CACHE["plan"] = _plan(list(T.cores), topo)
    plan = _CACHE["plan"]
    ext = plan["ext"]
    if core not in ext:
        return
    rank = ext.index(core)
    works = rank < N
    S = T.sem
    Relu, Copy = ActivationFunctionType.Relu, ActivationFunctionType.Copy

    def blk(j):
        return slice(NC * j, NC * (j + 1))

    if works:
        g.sync.dma_start(T.xb[:], T.x[:]).then_inc(S.lx, 16)
        g.scalar.dma_start(T.w1b[:, 0:TW], T.w1[:, 0:TW]).then_inc(S.la, 16)
        g.sync.dma_start(T.w1b[:, TW:2 * TW], T.w1[:, TW:2 * TW]).then_inc(S.lb, 16)
        g.sync.wait_ge(S.lx, 16)
        g.sync.wait_ge(S.la, 16)
        g.sync.wait_ge(S.lb, 16)
        g.sync.dma_start(T.w2b[:], T.w2[:]).then_inc(S.lw, 16)

        g.vector.wait_ge(S.lx, 16)
        g.vector.quantize_mx(T.xq[:], T.xs[:], T.xb[:]).then_inc(S.qx, 1)
        g.vector.wait_ge(S.la, 16)
        g.vector.quantize_mx(T.w1q[:, 0:NC], T.w1s[:, 0:NC], T.w1b[:, 0:TW]).then_inc(S.qa, 1)
        g.vector.wait_ge(S.lb, 16)
        g.vector.quantize_mx(T.w1q[:, NC:2 * NC], T.w1s[:, NC:2 * NC], T.w1b[:, TW:2 * TW]).then_inc(S.qb, 1)

        g.tensor.wait_ge(S.qx, 1)
        g.tensor.wait_ge(S.qa, 1)
        g.tensor.matmul_mx(T.ps[:, 0:NC], T.w1q[:, 0:NC], T.w1s[:, 0:NC], T.xq[:], T.xs[:], True, True).then_inc(S.z0, 1)
        g.tensor.wait_ge(S.qb, 1)
        g.tensor.matmul_mx(T.ps[:, BANK:BANK + NC], T.w1q[:, NC:2 * NC], T.w1s[:, NC:2 * NC], T.xq[:], T.xs[:], True, True).then_inc(S.z1, 1)

        g.scalar.wait_ge(S.z0, 1)
        g.scalar.activation(T.hb[:, 0:TW:4], T.ps[:, 0:NC], Relu, scale=C).then_inc(S.act, 1)
        g.scalar.activation(T.hb[:, 1:TW:4], T.ps[:, 0:NC], Relu, scale=-C).then_inc(S.act, 1)
        g.vector.wait_ge(S.z1, 1)
        g.vector.tensor_scalar(T.hb[:, 2:TW:4], T.ps[:, BANK:BANK + NC], C, 0.0, AluOpType.mult, AluOpType.max).then_inc(S.act, 1)
        g.vector.tensor_scalar(T.hb[:, 3:TW:4], T.ps[:, BANK:BANK + NC], -C, 0.0, AluOpType.mult, AluOpType.max).then_inc(S.act, 1)
        g.vector.wait_ge(S.act, 4)
        g.vector.quantize_mx(T.hq[:, blk(rank)], T.hs[:, blk(rank)], T.hb[:]).then_inc(S.hqd, 1)
        g.vector.wait_ge(S.lw, 16)
        g.vector.quantize_mx(T.w2q[:], T.w2s[:], T.w2b[:]).then_inc(S.qw, 1)

    sent = [0]

    def send(j, grp, codes):
        mask = plan["eng"][rank]
        sem = S["c%d" % j] if codes else S["p%d" % j]

        def view():
            return T.hq[:, blk(j)].bitcast(dt.uint8) if codes else T.hs[:, blk(j)]

        where = [topo.addr(ext[r], core) for r in grp]
        if len(grp) == 1:
            g.remote_dma(out_ap=view(), in_ap=view(), remote_sem=sem, local_sem=S.sent,
                         pid=where[0][1], routing_id=where[0][0], dma_engine_mask=mask)
        else:
            g.remote_dma_fused([RemoteDMATransfer(dst_ids=[DstId(rid=a, pnc=p) for a, p in where], dma_engine_mask=mask,
                                                  remote_sem=sem, srcs=[view()], dsts=[view() for _ in grp], alu_op=0)],
                               local_sem=S.sent)
        sent[0] += _engines(mask)

    def landed(j):
        return _engines(plan["eng"][plan["src"][(rank, j)][0]])

    if plan["own"][rank]:
        g.wait_ge(S.hqd, 1)
    for grp in plan["own"][rank]:
        send(rank, grp, False)
        send(rank, grp, True)
    for j, grp in plan["fwd"][rank]:
        g.wait_ge(S["p%d" % j], landed(j))
        send(j, grp, False)
        g.wait_ge(S["c%d" % j], landed(j))
        send(j, grp, True)

    stores = {"sts": 0, "sta": 0}
    if works:
        g.tensor.wait_ge(S.qw, 1)
        for k, j in enumerate(plan["order"][rank]):
            bank = (k + 2) % 8
            out = T.ps[:, BANK * bank:BANK * bank + NC]
            if j == rank:
                g.tensor.wait_ge(S.hqd, 1)
            else:
                g.tensor.wait_ge(S["p%d" % j], landed(j))
                g.tensor.wait_ge(S["c%d" % j], landed(j))
            g.tensor.matmul_mx(out, T.w2q[:], T.w2s[:], T.hq[:, blk(j)], T.hs[:, blk(j)], True, True).then_inc(S["m%d" % k], 1)
            if k % 2 == 0:
                g.vector.wait_ge(S["m%d" % k], 1)
                g.vector.tensor_copy(T.ysb[:, blk(j)], out).then_inc(S["v%d" % k], 1)
                g.sync.wait_ge(S["v%d" % k], 1)
                g.sync.dma_start(T.y[:, blk(j)], T.ysb[:, blk(j)]).then_inc(S.sts, 16)
                stores["sts"] += 16
            else:
                g.scalar.wait_ge(S["m%d" % k], 1)
                g.scalar.activation(T.ysb[:, blk(j)], out, Copy).then_inc(S["v%d" % k], 1)
                g.scalar.wait_ge(S["v%d" % k], 1)
                g.scalar.dma_start(T.y[:, blk(j)], T.ysb[:, blk(j)]).then_inc(S.sta, 16)
                stores["sta"] += 16

    if sent[0]:
        g.wait_ge(S.sent, sent[0])
    for name, total in stores.items():
        if total:
            g.wait_ge(S[name], total)
